import numpy as np
import ml_dtypes


def mxq(x, axis, fmt="e4m3"):
    dtype, down = {"e4m3": (ml_dtypes.float8_e4m3fn, 7), "e5m2": (ml_dtypes.float8_e5m2, 14)}[fmt]
    v = np.moveaxis(np.asarray(x, np.float32).astype(ml_dtypes.bfloat16).astype(np.float64), axis, -1)
    blocks = v.reshape(v.shape[:-1] + (-1, 32))
    amax = np.abs(blocks).max(-1, keepdims=True)
    byte = np.maximum(np.where(amax > 0, np.frexp(amax)[1] - 1 + 127, 0) - down, 1)
    scale = np.exp2(byte - 127.0)
    codes = (blocks / scale).astype(np.float32).astype(dtype).astype(np.float64)
    return np.moveaxis((codes * scale).reshape(v.shape), -1, axis)


WIDE = False


def mx_kscale(k):
    if not WIDE:
        return np.ones(k)
    levels = np.array([10, -10, 5, -5, 0])
    if k % 512:
        return np.exp2(np.random.permutation(np.resize(levels, k // 32))).repeat(32)
    a = np.empty((k // 512, 16))
    for p in range(k // 512):
        a[p, :8] = np.random.permutation(np.resize(levels, 8))
        for g in range(8):
            far = levels[np.abs(levels - a[p, g]) >= 10]
            a[p, g + 8] = far[np.random.randint(len(far))]
    return np.exp2(a.ravel()).repeat(32)


def f64(x):
    return np.asarray(x).astype(np.float64)


def striped(idx):
    return np.tile(idx.reshape(-1, 16).T, (8, 1)).astype(np.uint16)


def unstriped(offs):
    return offs[:16].T.reshape(-1).astype(np.int64)


def striped8(idx):
    return np.concatenate([x.reshape(-1, 16).T for x in idx]).astype(np.uint16)


def runs(offs, k):
    lists = np.stack([offs[16 * r : 16 * r + 16].T.reshape(-1) for r in range(8)]).astype(np.int64)
    return lists[np.arange(k) % 512 // 64]


def pack_weight(w):
    k, n = w.shape
    w = f64(np.asarray(w, np.float32).astype(ml_dtypes.bfloat16)).reshape(k // 32, 32, n)
    amax = np.abs(w).max(1)
    byte = np.clip(np.where(amax > 0, np.frexp(amax)[1] - 1 + 127 - 7, 1), 1, 254)
    scaled = (w * np.exp2(127.0 - byte)[:, None, :]).reshape(k, n).astype(np.float32)
    words = np.ascontiguousarray(scaled.reshape(k // 512, 128, 4, n).transpose(0, 1, 3, 2)).astype(ml_dtypes.float8_e4m3fn).view(np.uint8)
    return words, np.ascontiguousarray(byte.astype(np.uint8).reshape(k // 512, 16, n))


def unpack_weight(words, scales):
    g, p, n, _ = words.shape
    vals = np.ascontiguousarray(words).view(ml_dtypes.float8_e4m3fn).astype(np.float64) * np.repeat(np.exp2(scales.astype(np.float64) - 127.0), 8, axis=1)[..., None]
    return vals.transpose(0, 1, 3, 2).reshape(g * 512, n)


K, T, S, N, H, W = 512, 2048, 512, 512, 512, 256


def setup_inputs():
    n = np.random.standard_normal
    s = mx_kscale(K)[:, None]
    u = mx_kscale(S)
    packed_xT = pack_weight(n((K, T)) * s)
    return {
        "x_words": packed_xT[0],
        "x_scales": packed_xT[1],
        "wa": (n((K, H)) / np.sqrt(K) / s).astype(np.float32),
        "wb": (n((K, H)) / np.sqrt(K) / s).astype(np.float32),
        "gt": (np.random.uniform(0.5, 1.5, (S, 1)) * u[:, None]).astype(np.float32),
        "w1": (n((S, N)) / np.sqrt(S) / u[:, None]).astype(np.float32),
        "offs": striped(np.random.permutation(T)[:S]),
        "two": striped(np.random.permutation(T)[:S]),
        "n1": striped8(np.stack([np.random.permutation(H)[:W] for _ in range(8)])),
        "n2": striped8(np.stack([np.random.permutation(H)[:W] for _ in range(8)])),
        "n3": striped8(np.stack([np.random.permutation(H) for _ in range(8)])),
        "n4": striped8(np.stack([np.random.permutation(H) for _ in range(8)])),
    }


def reference(x_words, x_scales, wa, wb, gt, w1, offs, two, n1, n2, n3, n4):
    x_two = unpack_weight(x_words, x_scales)[:, unstriped(two)]
    d = x_two.T @ mxq(f64(wb), 0, "e4m3")
    xq = unpack_weight(x_words, x_scales)[:, unstriped(offs)]
    y = xq.T @ mxq(f64(wa), 0, "e4m3")
    ra = d[np.arange(S)[:, None], runs(n2, S)] - (0.5 * (y[np.arange(S)[:, None], runs(n1, S)]))
    ds = y.copy()
    ds[np.arange(S)[:, None], runs(n1, S)] = ra
    z = f64(gt) * ds
    h = mxq(f64(w1), 0, "e4m3").T @ mxq(z, 0, "e4m3")
    return (h - (h[np.arange(N)[:, None], runs(n3, N)])) / (np.abs(h[np.arange(N)[:, None], runs(n4, N)] - h) + 0.5)

@@ -1,0 +1,254 @@
+from contextlib import ExitStack
+
+import concourse.mybir as mybir
+
+K, T, S, N, H, W = 512, 2048, 512, 512, 512, 256
+FLOPS = 3 * 2 * 512 * 512 * 512
+
+F32 = mybir.dt.float32
+BF16 = mybir.dt.bfloat16
+U32 = mybir.dt.uint32
+I32 = mybir.dt.int32
+U16 = mybir.dt.uint16
+U8 = mybir.dt.uint8
+FP8X4 = mybir.dt.float8_e4m3fn_x4
+ALU = mybir.AluOpType
+ACT = mybir.ActivationFunctionType
+
+P = 128
+PACK = 4
+HALF = H // 2
+
+
+def tile_picked_twtputbfrac_none_p_kernel(
+    tc, x_words, x_scales, wa, wb, gt, w1, offs, two, n1, n2, n3, n4, out
+):
+    nc = tc.nc
+    with ExitStack() as ctx:
+        keep = ctx.enter_context(tc.tile_pool(name="keep", bufs=1))
+        ring = ctx.enter_context(tc.tile_pool(name="ring", bufs=2))
+        psum = ctx.enter_context(tc.psum_pool(name="psum", bufs=8))
+
+        def load_list(src, name):
+            tile = keep.tile(list(src.shape), U16, name=name)
+            nc.sync.dma_start(tile[:], src)
+            return tile
+
+        table_scales = keep.tile([P, T], U8, name="table_scales", align_bytes=64)
+        nc.vector.memset(table_scales[:].bitcast(I32), 0)
+        h_win = [keep.tile([P, 2 * H], F32, name="h_win%d" % u) for u in range(PACK)]
+
+        offs_sb = load_list(offs, "offs_sb")
+        two_sb = load_list(two, "two_sb")
+        for q in range(4):
+            nc.scalar.dma_start(
+                table_scales[32 * q : 32 * q + 4, :].bitcast(I32), x_scales[0, 4 * q : 4 * q + 4, :].bitcast(I32)
+            )
+        table_words = keep.tile([P, T], I32, name="table_words", align_bytes=64)
+        nc.sync.dma_start(table_words[:], x_words[0].rearrange("p n t -> p (n t)").bitcast(I32))
+
+        warm = keep.tile([P, 2], F32, name="warm")
+        nc.vector.memset(warm[:, 0:1], 1.0)
+        nc.scalar.activation(warm[:, 1:2], warm[:, 0:1], ACT.Abs_reciprocal_sqrt)
+
+        def load_weight_half(w, half, name):
+            raw = keep.tile([P, PACK, HALF], F32, name=name)
+            nc.sync.dma_start(raw[:], w.rearrange("(p t) j -> p t j", t=PACK)[:, :, half * HALF : (half + 1) * HALF])
+            return raw
+
+        wa_raw = [load_weight_half(wa, half, "wa_raw%d" % half) for half in range(2)]
+        gt_sb = keep.tile([P, PACK], F32, name="gt_sb")
+        for e in range(4):
+            nc.sync.dma_start(
+                gt_sb[e:P:4, :], gt.rearrange("(c t e) o -> e c (t o)", t=PACK, e=4)[e], allow_slow_non_contiguous=True
+            )
+        n1_sb = load_list(n1, "n1_sb")
+        wb_raw = [load_weight_half(wb, half, "wb_raw%d" % half) for half in range(2)]
+        n2_sb = load_list(n2, "n2_sb")
+        w1_raw = keep.tile([P, PACK, N], F32, name="w1_raw")
+        for e in range(4):
+            nc.sync.dma_start(w1_raw[e:P:4, :, :], w1.rearrange("(c t e) m -> e c t m", t=PACK, e=4)[e])
+        n3_sb = load_list(n3, "n3_sb")
+        n4_sb = load_list(n4, "n4_sb")
+
+        def pick_words(lst, name):
+            words = keep.tile([P, S], U32, name=name, align_bytes=64)
+            nc.vector.tensor_copy(
+                words[:].rearrange("p (t c e) -> p c t e", t=PACK, e=4), table_words[:].bitcast(U32).indirect(lst[:])
+            )
+            return words
+
+        def pick_scales(lst, name):
+            picked = keep.tile([P, S], U8, name=name + "_list", align_bytes=64)
+            nc.vector.tensor_copy(picked[:], table_scales[:].indirect(lst[:]))
+            return picked
+
+        def deal_scales(picked, name):
+            dealt = keep.tile([P, S], U8, name=name, align_bytes=64)
+            nc.vector.tensor_copy(
+                dealt[:].bitcast(I32).rearrange("p (t c) -> p t c", t=PACK),
+                picked[:].bitcast(I32).rearrange("p (c t) -> p t c", t=PACK),
+            )
+            return dealt
+
+        def weave(raw, name, copy):
+            grouped = keep.tile([P, HALF, PACK], BF16, name=name, align_bytes=64)
+            copy(
+                grouped[:].rearrange("p (c i) t -> p c t i", i=4), raw[:].rearrange("p t (c i) -> p c t i", i=4)
+            )
+            return grouped
+
+        def mx_tiles(name):
+            codes = keep.tile([P, H], U32, name=name + "_codes", align_bytes=64)
+            scales = keep.tile([P, H], U8, name=name + "_scales", align_bytes=64)
+            return codes, scales
+
+        def quantize(mx, cols, grouped):
+            nc.vector.quantize_mx(out=mx[0][:, cols].bitcast(FP8X4), scales=mx[1][:, cols], in_=grouped)
+
+        def product(acc, stationary, t, moving, cols):
+            rows = slice(t * P, (t + 1) * P)
+            nc.tensor.matmul_mx(
+                out=acc[:, cols],
+                lhsT=stationary[0][:, rows].bitcast(FP8X4),
+                lhsT_scale=stationary[1][:, rows],
+                rhs=moving[0][:, cols].bitcast(FP8X4),
+                rhs_scale=moving[1][:, cols],
+                start=True,
+                stop=True,
+            )
+
+        halves = [slice(half * HALF, (half + 1) * HALF) for half in range(2)]
+
+        def flat(grouped):
+            return grouped.rearrange("p j t -> p (j t)")
+
+        xo_picked = pick_scales(offs_sb, "xo_scales")
+        xt_picked = pick_scales(two_sb, "xt_scales")
+        xo_dealt = deal_scales(xo_picked, "xo_scales")
+        xt_dealt = deal_scales(xt_picked, "xt_scales")
+        xo = (pick_words(offs_sb, "xo_words"), xo_dealt)
+        xt = (pick_words(two_sb, "xt_words"), xt_dealt)
+
+        order = [1, 0, 3, 2]
+        whole = slice(0, H)
+
+        def project(picked, raws, weavers, name):
+            mx = mx_tiles(name)
+            accs = {t: psum.tile([P, H], F32, name="acc") for t in order}
+            for half in range(2):
+                grouped = weave(raws[half], name + "_grouped%d" % half, weavers[half])
+                quantize(mx, halves[half], flat(grouped[:]))
+                product(accs[order[0]], picked, order[0], mx, halves[half])
+            product(accs[order[1]], picked, order[1], mx, whole)
+            return accs, mx
+
+        y_acc, wa_mx = project(xo, wa_raw, [nc.scalar.copy, nc.scalar.copy], "wa")
+        d_acc, wb_mx = project(xt, wb_raw, [nc.scalar.copy, nc.vector.tensor_copy], "wb")
+        for t in order[2:]:
+            product(y_acc[t], xo, t, wa_mx, whole)
+            product(d_acc[t], xt, t, wb_mx, whole)
+
+        ds = [keep.tile([P, 2 * H if t % 2 == 0 else H], F32, name="ds%d" % t) for t in range(PACK)]
+        d_sb = [keep.tile([P, H], F32, name="d_sb%d" % t) for t in range(PACK)]
+        own = [keep.tile([P, W], F32, name="own%d" % t) for t in range(PACK)]
+        other = [keep.tile([P, W], F32, name="other%d" % t) for t in range(PACK)]
+        w1_grouped = keep.tile([P, PACK, P, PACK], BF16, name="w1_grouped", align_bytes=64)
+        w1_mx = mx_tiles("w1")
+        z_grouped = keep.tile([P, H, PACK], BF16, name="z_grouped", align_bytes=64)
+        z_mx = mx_tiles("z")
+
+        def leave_y(t):
+            nc.scalar.activation(ds[t][:, whole], y_acc[t][:], ACT.Copy, scale=gt_sb[:, t : t + 1])
+
+        def leave_d(t):
+            nc.scalar.activation(d_sb[t][:], d_acc[t][:], ACT.Copy, scale=gt_sb[:, t : t + 1])
+
+        def fetch_own(t):
+            nc.vector.tensor_scalar(own[t][:], ds[t][:].indirect(n1_sb[:]), -0.5, 0.0, ALU.mult, ALU.add)
+
+        def fetch_other(t):
+            nc.vector.tensor_copy(other[t][:], d_sb[t][:].indirect(n2_sb[:]))
+
+        def put(t):
+            nc.vector.tensor_tensor(ds[t][:].indirect(n1_sb[:]), other[t][:], own[t][:], ALU.add)
+
+        def join(t):
+            nc.scalar.copy(ds[t - 1][:, H:], ds[t][:])
+
+        def weave_pair(t, cols, copy):
+            copy(z_grouped[:, cols, t : t + 2], ds[t][:].rearrange("p (a j) -> p j a", a=2)[:, cols, :])
+
+        leave_y(order[0])
+        leave_y(order[1])
+        leave_d(order[0])
+        leave_d(order[1])
+        leave_y(order[2])
+        leave_d(order[2])
+        leave_y(order[3])
+        fetch_own(order[0])
+        for step, t in enumerate(order):
+            fetch_other(t)
+            if step + 1 < PACK:
+                fetch_own(order[step + 1])
+            else:
+                quantize(w1_mx, slice(0, N), w1_grouped[:].rearrange("p u m t -> p (u m t)"))
+            put(t)
+            if t % 2 == 1:
+                join(t)
+            if step == 0:
+                leave_d(order[-1])
+                for quarter in range(4):
+                    ms = slice(quarter * 32, (quarter + 1) * 32)
+                    nc.scalar.copy(
+                        w1_grouped[:].rearrange("p u m t -> p m t u")[:, ms],
+                        w1_raw[:].rearrange("p t (m u) -> p m t u", u=PACK)[:, ms],
+                    )
+            if step == 1:
+                weave_pair(t, whole, nc.scalar.copy)
+        for cols in halves:
+            weave_pair(order[-1], cols, nc.vector.tensor_copy)
+        first_acc = [psum.tile([P, H], F32, name="acc") for cols in halves]
+        h_acc = [None] + [psum.tile([P, H], F32, name="acc") for u in range(1, PACK)]
+        for half, cols in enumerate(halves):
+            quantize(z_mx, cols, flat(z_grouped[:, cols, :]))
+            product(first_acc[half], w1_mx, 0, z_mx, cols)
+        for u in range(1, PACK):
+            product(h_acc[u], w1_mx, u, z_mx, whole)
+
+        out_rows = out.rearrange("(p u) j -> u p j", u=PACK)
+        h_neg = [keep.tile([P, H], F32, name="h_plain%d" % u) for u in range(PACK)]
+        gap = [keep.tile([P, H], F32, name="gap%d" % u) for u in range(PACK)]
+        num = [keep.tile([P, H], F32, name="num%d" % u) for u in range(PACK)]
+        inv = [keep.tile([P, H], F32, name="inv%d" % u) for u in range(PACK)]
+
+        def leave_bank(u, acc, cols):
+            nc.scalar.activation(h_win[u][:, cols], acc[:, cols], ACT.Copy, scale=-1.0)
+            nc.scalar.activation(h_neg[u][:, cols], acc[:, cols], ACT.Copy, scale=-1.0)
+
+        def fetch(u):
+            nc.vector.tensor_tensor(gap[u][:], h_win[u][:].indirect(n4_sb[:]), h_neg[u][:], ALU.subtract)
+            nc.vector.tensor_tensor(num[u][:], h_win[u][:].indirect(n3_sb[:]), h_neg[u][:], ALU.subtract)
+
+        def invert(u):
+            mag = ring.tile([P, H], F32, name="mag")
+            nc.scalar.activation(mag[:], gap[u][:], ACT.Abs)
+            root = ring.tile([P, H], F32, name="root")
+            nc.scalar.activation(root[:], mag[:], ACT.Abs_reciprocal_sqrt, bias=0.5)
+            nc.scalar.activation(inv[u][:], root[:], ACT.Square)
+
+        def finish(u):
+            res = ring.tile([P, H], F32, name="res")
+            nc.vector.tensor_tensor(res[:], num[u][:], inv[u][:], ALU.mult)
+            nc.sync.dma_start(out_rows[u], res[:])
+
+        for half, cols in enumerate(halves):
+            leave_bank(0, first_acc[half], cols)
+        for u in range(PACK):
+            if u + 1 < PACK:
+                leave_bank(u + 1, h_acc[u + 1], whole)
+            fetch(u)
+            invert(u)
+            if u > 0:
+                finish(u - 1)
+        finish(PACK - 1)

@@ -41,7 +41,7 @@ def tile_picked_twtputbfrac_none_p_kernel(
         offs_sb = load_list(offs, "offs_sb")
         two_sb = load_list(two, "two_sb")
         for q in range(4):
-            nc.scalar.dma_start(
+            nc.sync.dma_start(
                 table_scales[32 * q : 32 * q + 4, :].bitcast(I32), x_scales[0, 4 * q : 4 * q + 4, :].bitcast(I32)
             )
         table_words = keep.tile([P, T], I32, name="table_words", align_bytes=64)
@@ -52,16 +52,14 @@ def tile_picked_twtputbfrac_none_p_kernel(
         nc.scalar.activation(warm[:, 1:2], warm[:, 0:1], ACT.Abs_reciprocal_sqrt)
 
         def load_weight_half(w, half, name):
-            raw = keep.tile([P, PACK, HALF], F32, name=name)
+            raw = keep.tile([P, PACK, HALF], F32, name=name, tag=name, align_bytes=64)
             nc.sync.dma_start(raw[:], w.rearrange("(p t) j -> p t j", t=PACK)[:, :, half * HALF : (half + 1) * HALF])
             return raw
 
         wa_raw = [load_weight_half(wa, half, "wa_raw%d" % half) for half in range(2)]
-        gt_sb = keep.tile([P, PACK], F32, name="gt_sb")
+        gt_sb = keep.tile([P, 13], F32, name="gt_sb")
         for e in range(4):
-            nc.sync.dma_start(
-                gt_sb[e:P:4, :], gt.rearrange("(c t e) o -> e c (t o)", t=PACK, e=4)[e], allow_slow_non_contiguous=True
-            )
+            nc.sync.dma_start(gt_sb[e:P:4, :], gt.rearrange("(c x) o -> c (x o)", x=16)[:, e : e + 13])
         n1_sb = load_list(n1, "n1_sb")
         wb_raw = [load_weight_half(wb, half, "wb_raw%d" % half) for half in range(2)]
         n2_sb = load_list(n2, "n2_sb")
@@ -92,7 +90,7 @@ def tile_picked_twtputbfrac_none_p_kernel(
             return dealt
 
         def weave(raw, name, copy):
-            grouped = keep.tile([P, HALF, PACK], BF16, name=name, align_bytes=64)
+            grouped = keep.tile([P, HALF, PACK], BF16, name=name, tag=name, align_bytes=64)
             copy(
                 grouped[:].rearrange("p (c i) t -> p c t i", i=4), raw[:].rearrange("p t (c i) -> p c t i", i=4)
             )
@@ -130,7 +128,7 @@ def tile_picked_twtputbfrac_none_p_kernel(
         xo = (pick_words(offs_sb, "xo_words"), xo_dealt)
         xt = (pick_words(two_sb, "xt_words"), xt_dealt)
 
-        order = [1, 0, 3, 2]
+        order = [1, 3, 0, 2]
         whole = slice(0, H)
 
         def project(picked, raws, weavers, name):
@@ -140,38 +138,44 @@ def tile_picked_twtputbfrac_none_p_kernel(
                 grouped = weave(raws[half], name + "_grouped%d" % half, weavers[half])
                 quantize(mx, halves[half], flat(grouped[:]))
                 product(accs[order[0]], picked, order[0], mx, halves[half])
-            product(accs[order[1]], picked, order[1], mx, whole)
             return accs, mx
 
-        y_acc, wa_mx = project(xo, wa_raw, [nc.scalar.copy, nc.scalar.copy], "wa")
+        y_acc, wa_mx = project(xo, wa_raw, [nc.scalar.copy, nc.vector.tensor_copy], "wa")
+        product(y_acc[0], xo, 0, wa_mx, whole)
         d_acc, wb_mx = project(xt, wb_raw, [nc.scalar.copy, nc.vector.tensor_copy], "wb")
-        for t in order[2:]:
-            product(y_acc[t], xo, t, wa_mx, whole)
-            product(d_acc[t], xt, t, wb_mx, whole)
+        product(y_acc[3], xo, 3, wa_mx, whole)
+        product(d_acc[3], xt, 3, wb_mx, whole)
+        product(y_acc[2], xo, 2, wa_mx, whole)
+        product(d_acc[0], xt, 0, wb_mx, whole)
+        product(d_acc[2], xt, 2, wb_mx, whole)
 
-        ds = [keep.tile([P, 2 * H if t % 2 == 0 else H], F32, name="ds%d" % t) for t in range(PACK)]
-        d_sb = [keep.tile([P, H], F32, name="d_sb%d" % t) for t in range(PACK)]
-        own = [keep.tile([P, W], F32, name="own%d" % t) for t in range(PACK)]
+        ds_tags = ["wb_grouped0", "wb_raw1", "wb_grouped1", "wb_raw0"]
+        ds = [
+            keep.tile([P, 2 * H if t % 2 == 0 else H], F32, name="ds%d" % t, tag=ds_tags[t], align_bytes=64)
+            for t in range(PACK)
+        ]
+        d_sb = [keep.tile([P, H], F32, name="d_sb%d" % t, tag="d_sb%d" % t, align_bytes=64) for t in range(PACK)]
+        own_all = keep.tile([P, PACK * W], F32, name="own_all")
+        own = [own_all[:, t * W : (t + 1) * W] for t in range(PACK)]
         other = [keep.tile([P, W], F32, name="other%d" % t) for t in range(PACK)]
-        w1_grouped = keep.tile([P, PACK, P, PACK], BF16, name="w1_grouped", align_bytes=64)
         w1_mx = mx_tiles("w1")
         z_grouped = keep.tile([P, H, PACK], BF16, name="z_grouped", align_bytes=64)
         z_mx = mx_tiles("z")
 
         def leave_y(t):
-            nc.scalar.activation(ds[t][:, whole], y_acc[t][:], ACT.Copy, scale=gt_sb[:, t : t + 1])
+            nc.scalar.activation(ds[t][:, whole], y_acc[t][:], ACT.Copy, scale=gt_sb[:, 4 * t : 4 * t + 1])
 
         def leave_d(t):
-            nc.scalar.activation(d_sb[t][:], d_acc[t][:], ACT.Copy, scale=gt_sb[:, t : t + 1])
+            nc.scalar.activation(d_sb[t][:], d_acc[t][:], ACT.Copy, scale=gt_sb[:, 4 * t : 4 * t + 1])
 
         def fetch_own(t):
-            nc.vector.tensor_scalar(own[t][:], ds[t][:].indirect(n1_sb[:]), -0.5, 0.0, ALU.mult, ALU.add)
+            nc.vector.tensor_scalar(own[t], ds[t][:].indirect(n1_sb[:]), -0.5, 0.0, ALU.mult, ALU.add)
 
         def fetch_other(t):
             nc.vector.tensor_copy(other[t][:], d_sb[t][:].indirect(n2_sb[:]))
 
         def put(t):
-            nc.vector.tensor_tensor(ds[t][:].indirect(n1_sb[:]), other[t][:], own[t][:], ALU.add)
+            nc.vector.tensor_tensor(ds[t][:].indirect(n1_sb[:]), other[t][:], own[t], ALU.add)
 
         def join(t):
             nc.scalar.copy(ds[t - 1][:, H:], ds[t][:])
@@ -179,33 +183,37 @@ def tile_picked_twtputbfrac_none_p_kernel(
         def weave_pair(t, cols, copy):
             copy(z_grouped[:, cols, t : t + 2], ds[t][:].rearrange("p (a j) -> p j a", a=2)[:, cols, :])
 
-        leave_y(order[0])
-        leave_y(order[1])
-        leave_d(order[0])
-        leave_d(order[1])
-        leave_y(order[2])
-        leave_d(order[2])
-        leave_y(order[3])
-        fetch_own(order[0])
-        for step, t in enumerate(order):
-            fetch_other(t)
-            if step + 1 < PACK:
-                fetch_own(order[step + 1])
-            else:
-                quantize(w1_mx, slice(0, N), w1_grouped[:].rearrange("p u m t -> p (u m t)"))
-            put(t)
-            if t % 2 == 1:
-                join(t)
-            if step == 0:
-                leave_d(order[-1])
-                for quarter in range(4):
-                    ms = slice(quarter * 32, (quarter + 1) * 32)
-                    nc.scalar.copy(
-                        w1_grouped[:].rearrange("p u m t -> p m t u")[:, ms],
-                        w1_raw[:].rearrange("p t (m u) -> p m t u", u=PACK)[:, ms],
-                    )
-            if step == 1:
-                weave_pair(t, whole, nc.scalar.copy)
+        leave_y(1)
+        leave_y(0)
+        leave_d(1)
+        leave_y(3)
+        leave_d(3)
+        leave_y(2)
+        fetch_own(1)
+        fetch_own(0)
+        fetch_other(1)
+        fetch_own(3)
+        put(1)
+        join(1)
+        leave_d(0)
+        leave_d(2)
+        fetch_other(3)
+        fetch_own(2)
+        put(3)
+        join(3)
+        w1_grouped = keep.tile([P, PACK, P, PACK], BF16, name="w1_grouped", tag="d_sb1", align_bytes=64)
+        for quarter in range(4):
+            ms = slice(quarter * 32, (quarter + 1) * 32)
+            nc.scalar.copy(
+                w1_grouped[:].rearrange("p u m t -> p m t u")[:, ms],
+                w1_raw[:].rearrange("p t (m u) -> p m t u", u=PACK)[:, ms],
+            )
+        fetch_other(0)
+        fetch_other(2)
+        put(0)
+        weave_pair(0, whole, nc.scalar.copy)
+        quantize(w1_mx, slice(0, N), w1_grouped[:].rearrange("p u m t -> p (u m t)"))
+        put(2)
         for cols in halves:
             weave_pair(order[-1], cols, nc.vector.tensor_copy)
         first_acc = [psum.tile([P, H], F32, name="acc") for cols in halves]

@@ -63,7 +63,7 @@ def tile_picked_twtputbfrac_none_p_kernel(
         n1_sb = load_list(n1, "n1_sb")
         wb_raw = [load_weight_half(wb, half, "wb_raw%d" % half) for half in range(2)]
         n2_sb = load_list(n2, "n2_sb")
-        w1_raw = keep.tile([P, PACK, N], F32, name="w1_raw")
+        w1_raw = keep.tile([P, PACK, N], F32, name="w1_raw", tag="w1_raw", align_bytes=64)
         for e in range(4):
             nc.sync.dma_start(w1_raw[e:P:4, :, :], w1.rearrange("(c t e) m -> e c t m", t=PACK, e=4)[e])
         n3_sb = load_list(n3, "n3_sb")
@@ -75,19 +75,6 @@ def tile_picked_twtputbfrac_none_p_kernel(
                 words[:].rearrange("p (t c e) -> p c t e", t=PACK, e=4), table_words[:].bitcast(U32).indirect(lst[:])
             )
             return words
-
-        def pick_scales(lst, name):
-            picked = keep.tile([P, S], U8, name=name + "_list", align_bytes=64)
-            nc.vector.tensor_copy(picked[:], table_scales[:].indirect(lst[:]))
-            return picked
-
-        def deal_scales(picked, name):
-            dealt = keep.tile([P, S], U8, name=name, align_bytes=64)
-            nc.vector.tensor_copy(
-                dealt[:].bitcast(I32).rearrange("p (t c) -> p t c", t=PACK),
-                picked[:].bitcast(I32).rearrange("p (c t) -> p t c", t=PACK),
-            )
-            return dealt
 
         def weave(raw, name, copy):
             grouped = keep.tile([P, HALF, PACK], BF16, name=name, tag=name, align_bytes=64)
@@ -121,12 +108,17 @@ def tile_picked_twtputbfrac_none_p_kernel(
         def flat(grouped):
             return grouped.rearrange("p j t -> p (j t)")
 
-        xo_picked = pick_scales(offs_sb, "xo_scales")
-        xt_picked = pick_scales(two_sb, "xt_scales")
-        xo_dealt = deal_scales(xo_picked, "xo_scales")
-        xt_dealt = deal_scales(xt_picked, "xt_scales")
-        xo = (pick_words(offs_sb, "xo_words"), xo_dealt)
-        xt = (pick_words(two_sb, "xt_words"), xt_dealt)
+        picked_scales = keep.tile([P, 2 * S], U8, name="picked_scales", align_bytes=64)
+        dealt_scales = keep.tile([P, 2 * S], U8, name="dealt_scales", align_bytes=64)
+        for a, lst in enumerate((offs_sb, two_sb)):
+            nc.vector.tensor_copy(picked_scales[:, a * S : (a + 1) * S], table_scales[:].indirect(lst[:]))
+        xo_words = pick_words(offs_sb, "xo_words")
+        nc.vector.tensor_copy(
+            dealt_scales[:].bitcast(I32).rearrange("p (a t c) -> p a t c", a=2, t=PACK),
+            picked_scales[:].bitcast(I32).rearrange("p (a c t) -> p a t c", a=2, t=PACK),
+        )
+        xo = (xo_words, dealt_scales[:, 0:S])
+        xt = (pick_words(two_sb, "xt_words"), dealt_scales[:, S:])
 
         order = [1, 3, 0, 2]
         whole = slice(0, H)
@@ -158,8 +150,6 @@ def tile_picked_twtputbfrac_none_p_kernel(
         own_all = keep.tile([P, PACK * W], F32, name="own_all")
         own = [own_all[:, t * W : (t + 1) * W] for t in range(PACK)]
         other = [keep.tile([P, W], F32, name="other%d" % t) for t in range(PACK)]
-        w1_mx = mx_tiles("w1")
-        z_grouped = keep.tile([P, H, PACK], BF16, name="z_grouped", align_bytes=64)
         z_mx = mx_tiles("z")
 
         def leave_y(t):
@@ -208,35 +198,47 @@ def tile_picked_twtputbfrac_none_p_kernel(
                 w1_grouped[:].rearrange("p u m t -> p m t u")[:, ms],
                 w1_raw[:].rearrange("p t (m u) -> p m t u", u=PACK)[:, ms],
             )
+        z_grouped = keep.tile([P, H, PACK], BF16, name="z_grouped", tag="w1_raw", align_bytes=64)
         fetch_other(0)
         fetch_other(2)
         put(0)
         weave_pair(0, whole, nc.scalar.copy)
-        quantize(w1_mx, slice(0, N), w1_grouped[:].rearrange("p u m t -> p (u m t)"))
+        w1_flat = w1_grouped[:].rearrange("p u m t -> p (u m t)")
+        w1_early = (
+            keep.tile([P, HALF], U32, name="w1_early_codes", align_bytes=64),
+            keep.tile([P, HALF], U8, name="w1_early_scales", align_bytes=64),
+        )
+        quantize(w1_early, halves[0], w1_flat[:, 0 : HALF * PACK])
         put(2)
-        for cols in halves:
-            weave_pair(order[-1], cols, nc.vector.tensor_copy)
+        weave_pair(2, slice(0, P), nc.scalar.copy)
+        weave_pair(2, slice(P, HALF), nc.vector.tensor_copy)
+        weave_pair(2, halves[1], nc.vector.tensor_copy)
         first_acc = [psum.tile([P, H], F32, name="acc") for cols in halves]
         h_acc = [None] + [psum.tile([P, H], F32, name="acc") for u in range(1, PACK)]
         for half, cols in enumerate(halves):
             quantize(z_mx, cols, flat(z_grouped[:, cols, :]))
-            product(first_acc[half], w1_mx, 0, z_mx, cols)
-        for u in range(1, PACK):
-            product(h_acc[u], w1_mx, u, z_mx, whole)
+            product(first_acc[half], w1_early, 0, z_mx, cols)
+        product(h_acc[1], w1_early, 1, z_mx, whole)
+        w1_late = (
+            keep.tile([P, HALF], U32, name="w1_late_codes", tag=ds_tags[2], align_bytes=64),
+            keep.tile([P, HALF], U8, name="w1_late_scales", align_bytes=64),
+        )
+        quantize(w1_late, halves[0], w1_flat[:, HALF * PACK :])
+        for u in range(2, PACK):
+            product(h_acc[u], w1_late, u - 2, z_mx, whole)
 
         out_rows = out.rearrange("(p u) j -> u p j", u=PACK)
         h_neg = [keep.tile([P, H], F32, name="h_plain%d" % u) for u in range(PACK)]
         gap = [keep.tile([P, H], F32, name="gap%d" % u) for u in range(PACK)]
-        num = [keep.tile([P, H], F32, name="num%d" % u) for u in range(PACK)]
         inv = [keep.tile([P, H], F32, name="inv%d" % u) for u in range(PACK)]
 
         def leave_bank(u, acc, cols):
             nc.scalar.activation(h_win[u][:, cols], acc[:, cols], ACT.Copy, scale=-1.0)
             nc.scalar.activation(h_neg[u][:, cols], acc[:, cols], ACT.Copy, scale=-1.0)
 
-        def fetch(u):
-            nc.vector.tensor_tensor(gap[u][:], h_win[u][:].indirect(n4_sb[:]), h_neg[u][:], ALU.subtract)
-            nc.vector.tensor_tensor(num[u][:], h_win[u][:].indirect(n3_sb[:]), h_neg[u][:], ALU.subtract)
+        def fetch(u, dst, lst, cols):
+            picks = lst[:, cols.start // 16 : cols.stop // 16]
+            nc.vector.tensor_tensor(dst[:, cols], h_win[u][:].indirect(picks), h_neg[u][:, cols], ALU.subtract)
 
         def invert(u):
             mag = ring.tile([P, H], F32, name="mag")
@@ -245,18 +247,37 @@ def tile_picked_twtputbfrac_none_p_kernel(
             nc.scalar.activation(root[:], mag[:], ACT.Abs_reciprocal_sqrt, bias=0.5)
             nc.scalar.activation(inv[u][:], root[:], ACT.Square)
 
-        def finish(u):
-            res = ring.tile([P, H], F32, name="res")
-            nc.vector.tensor_tensor(res[:], num[u][:], inv[u][:], ALU.mult)
-            nc.sync.dma_start(out_rows[u], res[:])
+        def finish(u, num, cols):
+            res = keep.tile([P, cols.stop - cols.start], F32, name="res%d_%d" % (u, cols.start))
+            nc.vector.tensor_tensor(res[:], num[:, cols], inv[u][:, cols], ALU.mult)
+            nc.sync.dma_start(out_rows[u][:, cols], res[:])
 
         for half, cols in enumerate(halves):
             leave_bank(0, first_acc[half], cols)
-        for u in range(PACK):
-            if u + 1 < PACK:
-                leave_bank(u + 1, h_acc[u + 1], whole)
-            fetch(u)
+        leave_bank(1, h_acc[1], whole)
+        for u in range(2, PACK):
+            nc.scalar.activation(h_win[u][:, whole], h_acc[u][:], ACT.Copy, scale=-1.0)
+            nc.sync.dma_start(h_neg[u][:], h_win[u][:, whole])
+
+        for cols in halves:
+            fetch(0, gap[0], n4_sb, cols)
+        invert(0)
+        num0 = keep.tile([P, H], F32, name="num0")
+        fetch(0, num0, n3_sb, whole)
+        fetch(1, gap[1], n4_sb, whole)
+        invert(1)
+        num = keep.tile([P, H], F32, name="num")
+        fetch(1, num, n3_sb, whole)
+        finish(0, num0, whole)
+        for u in range(2, PACK):
+            fetch(u, gap[u], n4_sb, whole)
             invert(u)
-            if u > 0:
-                finish(u - 1)
-        finish(PACK - 1)
+        finish(1, num, whole)
+        num = keep.tile([P, H], F32, name="num")
+        fetch(2, num, n3_sb, whole)
+        finish(2, num, whole)
+        num = keep.tile([P, H], F32, name="num")
+        for cols in halves:
+            fetch(3, num, n3_sb, cols)
+        for cols in halves:
+            finish(3, num, cols)

@@ -40,12 +40,14 @@ def tile_picked_twtputbfrac_none_p_kernel(
 
         offs_sb = load_list(offs, "offs_sb")
         two_sb = load_list(two, "two_sb")
+        n1_sb = load_list(n1, "n1_sb")
         for q in range(4):
             nc.sync.dma_start(
                 table_scales[32 * q : 32 * q + 4, :].bitcast(I32), x_scales[0, 4 * q : 4 * q + 4, :].bitcast(I32)
             )
         table_words = keep.tile([P, T], I32, name="table_words", align_bytes=64)
         nc.sync.dma_start(table_words[:], x_words[0].rearrange("p n t -> p (n t)").bitcast(I32))
+
 
         warm = keep.tile([P, 2], F32, name="warm")
         nc.vector.memset(warm[:, 0:1], 1.0)
@@ -57,11 +59,10 @@ def tile_picked_twtputbfrac_none_p_kernel(
             return raw
 
         wa_raw = [load_weight_half(wa, half, "wa_raw%d" % half) for half in range(2)]
+        wb_raw = [load_weight_half(wb, half, "wb_raw%d" % half) for half in range(2)]
         gt_sb = keep.tile([P, 13], F32, name="gt_sb")
         for e in range(4):
             nc.sync.dma_start(gt_sb[e:P:4, :], gt.rearrange("(c x) o -> c (x o)", x=16)[:, e : e + 13])
-        n1_sb = load_list(n1, "n1_sb")
-        wb_raw = [load_weight_half(wb, half, "wb_raw%d" % half) for half in range(2)]
         n2_sb = load_list(n2, "n2_sb")
         w1_raw = keep.tile([P, PACK, N], F32, name="w1_raw", tag="w1_raw", align_bytes=64)
         for e in range(4):
@@ -259,25 +260,12 @@ def tile_picked_twtputbfrac_none_p_kernel(
             nc.scalar.activation(h_win[u][:, whole], h_acc[u][:], ACT.Copy, scale=-1.0)
             nc.sync.dma_start(h_neg[u][:], h_win[u][:, whole])
 
-        for cols in halves:
-            fetch(0, gap[0], n4_sb, cols)
-        invert(0)
-        num0 = keep.tile([P, H], F32, name="num0")
-        fetch(0, num0, n3_sb, whole)
-        fetch(1, gap[1], n4_sb, whole)
-        invert(1)
-        num = keep.tile([P, H], F32, name="num")
-        fetch(1, num, n3_sb, whole)
-        finish(0, num0, whole)
-        for u in range(2, PACK):
-            fetch(u, gap[u], n4_sb, whole)
+        num = [keep.tile([P, H], F32, name="num%d" % u) for u in range(PACK)]
+        for u in range(PACK):
+            for cols in halves if u == 0 else [whole]:
+                fetch(u, gap[u], n4_sb, cols)
             invert(u)
-        finish(1, num, whole)
-        num = keep.tile([P, H], F32, name="num")
-        fetch(2, num, n3_sb, whole)
-        finish(2, num, whole)
-        num = keep.tile([P, H], F32, name="num")
-        for cols in halves:
-            fetch(3, num, n3_sb, cols)
-        for cols in halves:
-            finish(3, num, cols)
+            fetch(u, num[u], n3_sb, whole)
+        for u in range(PACK):
+            for cols in halves if u == PACK - 1 else [whole]:
+                finish(u, num[u], cols)

from contextlib import ExitStack

import concourse.mybir as mybir

K, T, S, N, H, W = 512, 2048, 512, 512, 512, 256
FLOPS = 3 * 2 * 512 * 512 * 512

F32 = mybir.dt.float32
BF16 = mybir.dt.bfloat16
U32 = mybir.dt.uint32
I32 = mybir.dt.int32
U16 = mybir.dt.uint16
U8 = mybir.dt.uint8
FP8X4 = mybir.dt.float8_e4m3fn_x4
ALU = mybir.AluOpType
ACT = mybir.ActivationFunctionType

P = 128
PACK = 4
HALF = H // 2


def tile_picked_twtputbfrac_none_p_kernel(
    tc, x_words, x_scales, wa, wb, gt, w1, offs, two, n1, n2, n3, n4, out
):
    nc = tc.nc
    with ExitStack() as ctx:
        keep = ctx.enter_context(tc.tile_pool(name="keep", bufs=1))
        ring = ctx.enter_context(tc.tile_pool(name="ring", bufs=2))
        psum = ctx.enter_context(tc.psum_pool(name="psum", bufs=8))

        def load_list(src, name):
            tile = keep.tile(list(src.shape), U16, name=name)
            nc.sync.dma_start(tile[:], src)
            return tile

        table_scales = keep.tile([P, T], U8, name="table_scales", align_bytes=64)
        nc.vector.memset(table_scales[:].bitcast(I32), 0)
        h_win = [keep.tile([P, 2 * H], F32, name="h_win%d" % u) for u in range(PACK)]

        offs_sb = load_list(offs, "offs_sb")
        two_sb = load_list(two, "two_sb")
        n1_sb = load_list(n1, "n1_sb")
        for q in range(4):
            nc.sync.dma_start(
                table_scales[32 * q : 32 * q + 4, :].bitcast(I32), x_scales[0, 4 * q : 4 * q + 4, :].bitcast(I32)
            )
        table_words = keep.tile([P, T], I32, name="table_words", align_bytes=64)
        nc.sync.dma_start(table_words[:], x_words[0].rearrange("p n t -> p (n t)").bitcast(I32))


        warm = keep.tile([P, 2], F32, name="warm")
        nc.vector.memset(warm[:, 0:1], 1.0)
        nc.scalar.activation(warm[:, 1:2], warm[:, 0:1], ACT.Abs_reciprocal_sqrt)

        def load_weight_half(w, half, name):
            raw = keep.tile([P, PACK, HALF], F32, name=name, tag=name, align_bytes=64)
            nc.sync.dma_start(raw[:], w.rearrange("(p t) j -> p t j", t=PACK)[:, :, half * HALF : (half + 1) * HALF])
            return raw

        wa_raw = [load_weight_half(wa, half, "wa_raw%d" % half) for half in range(2)]
        wb_raw = [load_weight_half(wb, half, "wb_raw%d" % half) for half in range(2)]
        gt_sb = keep.tile([P, 13], F32, name="gt_sb")
        for e in range(4):
            nc.sync.dma_start(gt_sb[e:P:4, :], gt.rearrange("(c x) o -> c (x o)", x=16)[:, e : e + 13])
        n2_sb = load_list(n2, "n2_sb")
        w1_raw = keep.tile([P, PACK, N], F32, name="w1_raw", tag="w1_raw", align_bytes=64)
        for e in range(4):
            nc.sync.dma_start(w1_raw[e:P:4, :, :], w1.rearrange("(c t e) m -> e c t m", t=PACK, e=4)[e])
        n3_sb = load_list(n3, "n3_sb")
        n4_sb = load_list(n4, "n4_sb")

        def pick_words(lst, name):
            words = keep.tile([P, S], U32, name=name, align_bytes=64)
            nc.vector.tensor_copy(
                words[:].rearrange("p (t c e) -> p c t e", t=PACK, e=4), table_words[:].bitcast(U32).indirect(lst[:])
            )
            return words

        def weave(raw, name, copy):
            grouped = keep.tile([P, HALF, PACK], BF16, name=name, tag=name, align_bytes=64)
            copy(
                grouped[:].rearrange("p (c i) t -> p c t i", i=4), raw[:].rearrange("p t (c i) -> p c t i", i=4)
            )
            return grouped

        def mx_tiles(name):
            codes = keep.tile([P, H], U32, name=name + "_codes", align_bytes=64)
            scales = keep.tile([P, H], U8, name=name + "_scales", align_bytes=64)
            return codes, scales

        def quantize(mx, cols, grouped):
            nc.vector.quantize_mx(out=mx[0][:, cols].bitcast(FP8X4), scales=mx[1][:, cols], in_=grouped)

        def product(acc, stationary, t, moving, cols):
            rows = slice(t * P, (t + 1) * P)
            nc.tensor.matmul_mx(
                out=acc[:, cols],
                lhsT=stationary[0][:, rows].bitcast(FP8X4),
                lhsT_scale=stationary[1][:, rows],
                rhs=moving[0][:, cols].bitcast(FP8X4),
                rhs_scale=moving[1][:, cols],
                start=True,
                stop=True,
            )

        halves = [slice(half * HALF, (half + 1) * HALF) for half in range(2)]

        def flat(grouped):
            return grouped.rearrange("p j t -> p (j t)")

        picked_scales = keep.tile([P, 2 * S], U8, name="picked_scales", align_bytes=64)
        dealt_scales = keep.tile([P, 2 * S], U8, name="dealt_scales", align_bytes=64)
        for a, lst in enumerate((offs_sb, two_sb)):
            nc.vector.tensor_copy(picked_scales[:, a * S : (a + 1) * S], table_scales[:].indirect(lst[:]))
        xo_words = pick_words(offs_sb, "xo_words")
        nc.vector.tensor_copy(
            dealt_scales[:].bitcast(I32).rearrange("p (a t c) -> p a t c", a=2, t=PACK),
            picked_scales[:].bitcast(I32).rearrange("p (a c t) -> p a t c", a=2, t=PACK),
        )
        xo = (xo_words, dealt_scales[:, 0:S])
        xt = (pick_words(two_sb, "xt_words"), dealt_scales[:, S:])

        order = [1, 3, 0, 2]
        whole = slice(0, H)

        def project(picked, raws, weavers, name):
            mx = mx_tiles(name)
            accs = {t: psum.tile([P, H], F32, name="acc") for t in order}
            for half in range(2):
                grouped = weave(raws[half], name + "_grouped%d" % half, weavers[half])
                quantize(mx, halves[half], flat(grouped[:]))
                product(accs[order[0]], picked, order[0], mx, halves[half])
            return accs, mx

        y_acc, wa_mx = project(xo, wa_raw, [nc.scalar.copy, nc.vector.tensor_copy], "wa")
        product(y_acc[0], xo, 0, wa_mx, whole)
        d_acc, wb_mx = project(xt, wb_raw, [nc.scalar.copy, nc.vector.tensor_copy], "wb")
        product(y_acc[3], xo, 3, wa_mx, whole)
        product(d_acc[3], xt, 3, wb_mx, whole)
        product(y_acc[2], xo, 2, wa_mx, whole)
        product(d_acc[0], xt, 0, wb_mx, whole)
        product(d_acc[2], xt, 2, wb_mx, whole)

        ds_tags = ["wb_grouped0", "wb_raw1", "wb_grouped1", "wb_raw0"]
        ds = [
            keep.tile([P, 2 * H if t % 2 == 0 else H], F32, name="ds%d" % t, tag=ds_tags[t], align_bytes=64)
            for t in range(PACK)
        ]
        d_sb = [keep.tile([P, H], F32, name="d_sb%d" % t, tag="d_sb%d" % t, align_bytes=64) for t in range(PACK)]
        own_all = keep.tile([P, PACK * W], F32, name="own_all")
        own = [own_all[:, t * W : (t + 1) * W] for t in range(PACK)]
        other = [keep.tile([P, W], F32, name="other%d" % t) for t in range(PACK)]
        z_mx = mx_tiles("z")

        def leave_y(t):
            nc.scalar.activation(ds[t][:, whole], y_acc[t][:], ACT.Copy, scale=gt_sb[:, 4 * t : 4 * t + 1])

        def leave_d(t):
            nc.scalar.activation(d_sb[t][:], d_acc[t][:], ACT.Copy, scale=gt_sb[:, 4 * t : 4 * t + 1])

        def fetch_own(t):
            nc.vector.tensor_scalar(own[t], ds[t][:].indirect(n1_sb[:]), -0.5, 0.0, ALU.mult, ALU.add)

        def fetch_other(t):
            nc.vector.tensor_copy(other[t][:], d_sb[t][:].indirect(n2_sb[:]))

        def put(t):
            nc.vector.tensor_tensor(ds[t][:].indirect(n1_sb[:]), other[t][:], own[t], ALU.add)

        def join(t):
            nc.scalar.copy(ds[t - 1][:, H:], ds[t][:])

        def weave_pair(t, cols, copy):
            copy(z_grouped[:, cols, t : t + 2], ds[t][:].rearrange("p (a j) -> p j a", a=2)[:, cols, :])

        leave_y(1)
        leave_y(0)
        leave_d(1)
        leave_y(3)
        leave_d(3)
        leave_y(2)
        fetch_own(1)
        fetch_own(0)
        fetch_other(1)
        fetch_own(3)
        put(1)
        join(1)
        leave_d(0)
        leave_d(2)
        fetch_other(3)
        fetch_own(2)
        put(3)
        join(3)
        w1_grouped = keep.tile([P, PACK, P, PACK], BF16, name="w1_grouped", tag="d_sb1", align_bytes=64)
        for quarter in range(4):
            ms = slice(quarter * 32, (quarter + 1) * 32)
            nc.scalar.copy(
                w1_grouped[:].rearrange("p u m t -> p m t u")[:, ms],
                w1_raw[:].rearrange("p t (m u) -> p m t u", u=PACK)[:, ms],
            )
        z_grouped = keep.tile([P, H, PACK], BF16, name="z_grouped", tag="w1_raw", align_bytes=64)
        fetch_other(0)
        fetch_other(2)
        put(0)
        weave_pair(0, whole, nc.scalar.copy)
        w1_flat = w1_grouped[:].rearrange("p u m t -> p (u m t)")
        w1_early = (
            keep.tile([P, HALF], U32, name="w1_early_codes", align_bytes=64),
            keep.tile([P, HALF], U8, name="w1_early_scales", align_bytes=64),
        )
        quantize(w1_early, halves[0], w1_flat[:, 0 : HALF * PACK])
        put(2)
        weave_pair(2, slice(0, P), nc.scalar.copy)
        weave_pair(2, slice(P, HALF), nc.vector.tensor_copy)
        weave_pair(2, halves[1], nc.vector.tensor_copy)
        first_acc = [psum.tile([P, H], F32, name="acc") for cols in halves]
        h_acc = [None] + [psum.tile([P, H], F32, name="acc") for u in range(1, PACK)]
        for half, cols in enumerate(halves):
            quantize(z_mx, cols, flat(z_grouped[:, cols, :]))
            product(first_acc[half], w1_early, 0, z_mx, cols)
        product(h_acc[1], w1_early, 1, z_mx, whole)
        w1_late = (
            keep.tile([P, HALF], U32, name="w1_late_codes", tag=ds_tags[2], align_bytes=64),
            keep.tile([P, HALF], U8, name="w1_late_scales", align_bytes=64),
        )
        quantize(w1_late, halves[0], w1_flat[:, HALF * PACK :])
        for u in range(2, PACK):
            product(h_acc[u], w1_late, u - 2, z_mx, whole)

        out_rows = out.rearrange("(p u) j -> u p j", u=PACK)
        h_neg = [keep.tile([P, H], F32, name="h_plain%d" % u) for u in range(PACK)]
        gap = [keep.tile([P, H], F32, name="gap%d" % u) for u in range(PACK)]
        inv = [keep.tile([P, H], F32, name="inv%d" % u) for u in range(PACK)]

        def leave_bank(u, acc, cols):
            nc.scalar.activation(h_win[u][:, cols], acc[:, cols], ACT.Copy, scale=-1.0)
            nc.scalar.activation(h_neg[u][:, cols], acc[:, cols], ACT.Copy, scale=-1.0)

        def fetch(u, dst, lst, cols):
            picks = lst[:, cols.start // 16 : cols.stop // 16]
            nc.vector.tensor_tensor(dst[:, cols], h_win[u][:].indirect(picks), h_neg[u][:, cols], ALU.subtract)

        def invert(u):
            mag = ring.tile([P, H], F32, name="mag")
            nc.scalar.activation(mag[:], gap[u][:], ACT.Abs)
            root = ring.tile([P, H], F32, name="root")
            nc.scalar.activation(root[:], mag[:], ACT.Abs_reciprocal_sqrt, bias=0.5)
            nc.scalar.activation(inv[u][:], root[:], ACT.Square)

        def finish(u, num, cols):
            res = keep.tile([P, cols.stop - cols.start], F32, name="res%d_%d" % (u, cols.start))
            nc.vector.tensor_tensor(res[:], num[:, cols], inv[u][:, cols], ALU.mult)
            nc.sync.dma_start(out_rows[u][:, cols], res[:])

        for half, cols in enumerate(halves):
            leave_bank(0, first_acc[half], cols)
        leave_bank(1, h_acc[1], whole)
        for u in range(2, PACK):
            nc.scalar.activation(h_win[u][:, whole], h_acc[u][:], ACT.Copy, scale=-1.0)
            nc.sync.dma_start(h_neg[u][:], h_win[u][:, whole])

        num = [keep.tile([P, H], F32, name="num%d" % u) for u in range(PACK)]
        for u in range(PACK):
            for cols in halves if u == 0 else [whole]:
                fetch(u, gap[u], n4_sb, cols)
            invert(u)
            fetch(u, num[u], n3_sb, whole)
        for u in range(PACK):
            for cols in halves if u == PACK - 1 else [whole]:
                finish(u, num[u], cols)
